import numpy as np
import ml_dtypes


def mxq(x, axis, fmt="e4m3"):
    dtype, down = {"e4m3": (ml_dtypes.float8_e4m3fn, 7), "e5m2": (ml_dtypes.float8_e5m2, 14)}[fmt]
    v = np.moveaxis(np.asarray(x, np.float32).astype(ml_dtypes.bfloat16).astype(np.float64), axis, -1)
    blocks = v.reshape(v.shape[:-1] + (-1, 32))
    amax = np.abs(blocks).max(-1, keepdims=True)
    byte = np.maximum(np.where(amax > 0, np.frexp(amax)[1] - 1 + 127, 0) - down, 1)
    scale = np.exp2(byte - 127.0)
    codes = (blocks / scale).astype(np.float32).astype(dtype).astype(np.float64)
    return np.moveaxis((codes * scale).reshape(v.shape), -1, axis)


WIDE = False


def mx_kscale(k):
    if not WIDE:
        return np.ones(k)
    levels = np.array([10, -10, 5, -5, 0])
    if k % 512:
        return np.exp2(np.random.permutation(np.resize(levels, k // 32))).repeat(32)
    a = np.empty((k // 512, 16))
    for p in range(k // 512):
        a[p, :8] = np.random.permutation(np.resize(levels, 8))
        for g in range(8):
            far = levels[np.abs(levels - a[p, g]) >= 10]
            a[p, g + 8] = far[np.random.randint(len(far))]
    return np.exp2(a.ravel()).repeat(32)


def f64(x):
    return np.asarray(x).astype(np.float64)


def striped(idx):
    return np.tile(idx.reshape(-1, 16).T, (8, 1)).astype(np.uint16)


def unstriped(offs):
    return offs[:16].T.reshape(-1).astype(np.int64)


def striped8(idx):
    return np.concatenate([x.reshape(-1, 16).T for x in idx]).astype(np.uint16)


def runs(offs, k):
    lists = np.stack([offs[16 * r : 16 * r + 16].T.reshape(-1) for r in range(8)]).astype(np.int64)
    return lists[np.arange(k) % 512 // 64]


def pack_weight(w):
    k, n = w.shape
    w = f64(np.asarray(w, np.float32).astype(ml_dtypes.bfloat16)).reshape(k // 32, 32, n)
    amax = np.abs(w).max(1)
    byte = np.clip(np.where(amax > 0, np.frexp(amax)[1] - 1 + 127 - 7, 1), 1, 254)
    scaled = (w * np.exp2(127.0 - byte)[:, None, :]).reshape(k, n).astype(np.float32)
    words = np.ascontiguousarray(scaled.reshape(k // 512, 128, 4, n).transpose(0, 1, 3, 2)).astype(ml_dtypes.float8_e4m3fn).view(np.uint8)
    return words, np.ascontiguousarray(byte.astype(np.uint8).reshape(k // 512, 16, n))


def unpack_weight(words, scales):
    g, p, n, _ = words.shape
    vals = np.ascontiguousarray(words).view(ml_dtypes.float8_e4m3fn).astype(np.float64) * np.repeat(np.exp2(scales.astype(np.float64) - 127.0), 8, axis=1)[..., None]
    return vals.transpose(0, 1, 3, 2).reshape(g * 512, n)


def sigmoid(v):
    return 1.0 / (1.0 + np.exp(-np.maximum(v, -700.0)))


K, T, S, N, H, W = 512, 2048, 512, 512, 512, 256


def setup_inputs():
    n = np.random.standard_normal
    s = mx_kscale(K)[:, None]
    u = mx_kscale(S)
    packed_xT = pack_weight(n((K, T)) * s)
    perm = np.stack([np.random.permutation(H) for _ in range(8)])
    perm2 = np.stack([np.random.permutation(H) for _ in range(8)])
    return {
        "x_words": packed_xT[0],
        "x_scales": packed_xT[1],
        "wa": (n((K, H)) / np.sqrt(K) / s).astype(np.float32),
        "gt": (np.random.uniform(0.5, 1.5, (S, 1)) * u[:, None]).astype(np.float32),
        "w1": (n((S, N)) / np.sqrt(S) / u[:, None]).astype(np.float32),
        "offs": striped(np.random.permutation(T)[:S]),
        "n1": striped8(perm[:, :W]),
        "n2": striped8(perm[:, W:]),
        "n3": striped8(perm2[:, :W]),
        "n4": striped8(perm2[:, W:]),
    }


def reference(x_words, x_scales, wa, gt, w1, offs, n1, n2, n3, n4):
    xq = unpack_weight(x_words, x_scales)[:, unstriped(offs)]
    y = xq.T @ mxq(f64(wa), 0, "e4m3")
    pa = y[np.arange(S)[:, None], runs(n1, S)]
    pb = y[np.arange(S)[:, None], runs(n2, S)]
    ra = np.maximum(pa, pb)
    ds = y.copy()
    ds[np.arange(S)[:, None], runs(n1, S)] = ra
    z = f64(gt) * ds
    h = mxq(f64(w1), 0, "e4m3").T @ mxq(z, 0, "e4m3")
    pb2 = h[np.arange(N)[:, None], runs(n4, N)]
    pa2 = h[np.arange(N)[:, None], runs(n3, N)]
    rb = pb2 * sigmoid(pb2 - pa2)
    ra2 = pa2 * sigmoid(pa2 - pb2)
    ds2 = np.zeros((N, H))
    ds2[np.arange(N)[:, None], runs(n3, N)] = ra2
    out = ds2.copy()
    out[np.arange(N)[:, None], runs(n4, N)] = rb
    return out

@@ -1,0 +1,223 @@
+from contextlib import ExitStack
+
+import concourse.mybir as mybir
+
+F32 = mybir.dt.float32
+BF16 = mybir.dt.bfloat16
+I32 = mybir.dt.int32
+U32 = mybir.dt.uint32
+U16 = mybir.dt.uint16
+U8 = mybir.dt.uint8
+FP8X4 = mybir.dt.float8_e4m3fn_x4
+ALU = mybir.AluOpType
+ACT = mybir.ActivationFunctionType
+
+P = 128
+PACK = 4
+T, S, H, N, W = 2048, 512, 512, 512, 256
+HALF = H // 2
+VECTOR_COLS = 96
+FLOPS = 2 * 512 * S * H + 2 * S * N * H
+
+
+def tile_picked_tokfillduel_none_p_kernel(tc, x_words, x_scales, wa, gt, w1, offs, n1, n2, n3, n4, out):
+    nc = tc.nc
+    with ExitStack() as ctx:
+        keep = ctx.enter_context(tc.tile_pool(name="keep", bufs=1))
+        rows = ctx.enter_context(tc.tile_pool(name="rows", bufs=3))
+        work = ctx.enter_context(tc.tile_pool(name="work", bufs=4))
+        psum = ctx.enter_context(tc.psum_pool(name="psum", bufs=8))
+
+        x_bytes = keep.tile([P, T], U8, align_bytes=64)
+        nc.vector.memset(x_bytes[:].bitcast(I32), 0)
+        for q in range(4):
+            nc.scalar.dma_start(x_bytes[32 * q : 32 * q + 4, :].bitcast(I32), x_scales[0, 4 * q : 4 * q + 4, :].bitcast(I32))
+        warm_in = keep.tile([P, 8], F32)
+        warm_out = keep.tile([P, 8], F32)
+        nc.vector.memset(warm_in[:], 0.0)
+        nc.scalar.activation(warm_out[:], warm_in[:], ACT.Sigmoid)
+
+        def load_list(dram, name):
+            tile = keep.tile(list(dram.shape), U16, name=name)
+            nc.sync.dma_start(tile[:], dram)
+            return tile
+
+        offs_sb = load_list(offs, "offs_sb")
+        x_codes = keep.tile([P, T], U32, align_bytes=64)
+        nc.sync.dma_start(x_codes[:].bitcast(I32), x_words[0].rearrange("p c r -> p (c r)").bitcast(I32))
+        wa_rows = wa.rearrange("(p j) n -> p j n", j=PACK)
+        wa_raw = []
+        for u in range(2):
+            raw = keep.tile([P, PACK, HALF], F32, name="wa_raw%d" % u)
+            nc.sync.dma_start(raw[:], wa_rows[:, :, u * HALF : (u + 1) * HALF])
+            wa_raw.append(raw)
+        n1_sb = load_list(n1, "n1_sb")
+        n2_sb = load_list(n2, "n2_sb")
+        gt_sb = keep.tile([P, PACK], F32)
+        nc.sync.dma_start(gt_sb[:], gt.rearrange("(p t) o -> p (t o)", t=PACK))
+        w1_raw = keep.tile([P, PACK, N], F32)
+        nc.sync.dma_start(w1_raw[:], w1.rearrange("(p j) n -> p j n", j=PACK))
+        n3_sb = load_list(n3, "n3_sb")
+        n4_sb = load_list(n4, "n4_sb")
+
+        tok_codes = keep.tile([P, S], U32, align_bytes=64)
+        nc.vector.tensor_copy(tok_codes[:].rearrange("p (t m) -> p m t", t=PACK), x_codes[:].indirect(offs_sb[:]))
+        picked_bytes = keep.tile([P, S], U8, align_bytes=64)
+        nc.vector.tensor_copy(picked_bytes[:], x_bytes[:].indirect(offs_sb[:]))
+        tok_bytes = keep.tile([P, S], U8, align_bytes=64)
+        nc.vector.tensor_copy(
+            tok_bytes[:].rearrange("p (t m) -> p m t", t=PACK), picked_bytes[:].rearrange("p (m t) -> p m t", t=PACK)
+        )
+
+        wa_codes = keep.tile([P, H], U32, align_bytes=64)
+        wa_bytes = keep.tile([P, H], U8, align_bytes=64)
+        for u in range(2):
+            grouped = keep.tile([P, HALF, PACK], BF16, align_bytes=64, name="wa_grouped%d" % u)
+            dst = grouped[:].rearrange("p (c i) j -> p c j i", i=4)
+            src = wa_raw[u][:].rearrange("p j (c i) -> p c j i", i=4)
+            cut = u * VECTOR_COLS // 4
+            nc.scalar.copy(dst[:, cut:], src[:, cut:])
+            if cut:
+                nc.vector.tensor_copy(dst[:, :cut], src[:, :cut])
+            cols = slice(u * HALF, (u + 1) * HALF)
+            nc.vector.quantize_mx(
+                out=wa_codes[:, cols].bitcast(FP8X4), scales=wa_bytes[:, cols], in_=grouped[:].rearrange("p n j -> p (n j)")
+            )
+
+        def product(dst, lhs_codes, lhs_bytes, rhs_codes, rhs_bytes, pieces):
+            width = H // pieces
+            for u in range(pieces):
+                cols = slice(u * width, (u + 1) * width)
+                acc = psum.tile([P, width], F32, name="acc")
+                nc.tensor.matmul_mx(
+                    out=acc[:],
+                    lhsT=lhs_codes.bitcast(FP8X4),
+                    lhsT_scale=lhs_bytes,
+                    rhs=rhs_codes[:, cols].bitcast(FP8X4),
+                    rhs_scale=rhs_bytes[:, cols],
+                    start=True,
+                    stop=True,
+                )
+                nc.scalar.copy(dst[:, cols], acc[:])
+
+        z_grouped = [keep.tile([P, HALF, PACK], BF16, align_bytes=64, name="z_grouped%d" % u) for u in range(2)]
+        w1_grouped = keep.tile([P, PACK, P, PACK], BF16, align_bytes=64)
+        w1_codes = keep.tile([P, N], U32, align_bytes=64)
+        w1_bytes = keep.tile([P, N], U8, align_bytes=64)
+
+        def quantize_w1(t0, t1):
+            cols = slice(t0 * P, t1 * P)
+            nc.vector.quantize_mx(
+                out=w1_codes[:, cols].bitcast(FP8X4),
+                scales=w1_bytes[:, cols],
+                in_=w1_grouped[:, t0:t1].rearrange("p t m j -> p (t m j)"),
+            )
+
+        order = (2, 0, 1, 3)
+        ys, pas, pbs, ras = {}, {}, {}, {}
+
+        def project(t, pieces):
+            cols = slice(t * P, (t + 1) * P)
+            ys[t] = rows.tile([P, H], F32, name="y")
+            product(ys[t], tok_codes[:, cols], tok_bytes[:, cols], wa_codes, wa_bytes, pieces)
+
+        def fetch(store, t, window, offsets, name):
+            store[t] = work.tile([P, W], F32, name=name)
+            nc.vector.tensor_copy(store[t][:], window[:].indirect(offsets[:]))
+
+        def larger(t):
+            ras[t] = work.tile([P, W], F32, name="ra")
+            nc.vector.tensor_tensor(ras[t][:], pas[t][:], pbs[t][:], ALU.max)
+
+        def put_larger(t):
+            nc.vector.tensor_copy(ys[t][:].indirect(n1_sb[:]), ras[t][:])
+
+        def weigh(t, vector_halves):
+            gain = gt_sb[:, t : t + 1]
+            for u in range(2):
+                src = ys[t][:, u * HALF : (u + 1) * HALF]
+                if u < vector_halves:
+                    nc.vector.tensor_scalar(z_grouped[u][:, :, t], src, gain, None, ALU.mult)
+                else:
+                    nc.scalar.activation(z_grouped[u][:, :, t], src, ACT.Copy, scale=gain)
+
+        a, b, c, d = order
+        project(a, 2)
+        project(b, 1)
+        project(c, 1)
+        fetch(pas, a, ys[a], n1_sb, "pa")
+        fetch(pbs, a, ys[a], n2_sb, "pb")
+        fetch(pas, b, ys[b], n1_sb, "pa")
+        larger(a)
+        fetch(pbs, b, ys[b], n2_sb, "pb")
+        put_larger(a)
+        weigh(a, 0)
+        project(d, 1)
+        for v in range(4):
+            ms = slice(v * P // 4, (v + 1) * P // 4)
+            nc.scalar.copy(
+                w1_grouped[:].rearrange("p t m j -> p m j t")[:, ms],
+                w1_raw[:].rearrange("p j (m t) -> p m j t", t=PACK)[:, ms],
+            )
+        larger(b)
+        fetch(pas, c, ys[c], n1_sb, "pa")
+        put_larger(b)
+        weigh(b, 0)
+        fetch(pbs, c, ys[c], n2_sb, "pb")
+        fetch(pas, d, ys[d], n1_sb, "pa")
+        larger(c)
+        fetch(pbs, d, ys[d], n2_sb, "pb")
+        put_larger(c)
+        weigh(c, 0)
+        larger(d)
+        quantize_w1(0, 1)
+        put_larger(d)
+        quantize_w1(1, 2)
+        weigh(d, 1)
+
+        z_codes = keep.tile([P, H], U32, align_bytes=64)
+        z_bytes = keep.tile([P, H], U8, align_bytes=64)
+        for u in range(2):
+            cols = slice(u * HALF, (u + 1) * HALF)
+            nc.vector.quantize_mx(
+                out=z_codes[:, cols].bitcast(FP8X4), scales=z_bytes[:, cols], in_=z_grouped[u][:].rearrange("p n j -> p (n j)")
+            )
+        quantize_w1(2, 4)
+
+        out_rows = out.rearrange("(p t) n -> t p n", t=PACK)
+        hs, pa2, pb2, sa, sb, res = {}, {}, {}, {}, {}, {}
+        for t in range(PACK):
+            cols = slice(t * P, (t + 1) * P)
+            hs[t] = work.tile([P, H], F32, name="h")
+            product(hs[t], w1_codes[:, cols], w1_bytes[:, cols], z_codes, z_bytes, 2 if t == 0 else 1)
+
+        def duel(t):
+            diff = work.tile([P, W], F32, name="diff")
+            sa[t] = work.tile([P, W], F32, name="sa")
+            sb[t] = work.tile([P, W], F32, name="sb")
+            nc.vector.tensor_tensor(diff[:], pa2[t][:], pb2[t][:], ALU.subtract)
+            nc.scalar.activation(sa[t][:], diff[:], ACT.Sigmoid)
+            nc.scalar.activation(sb[t][:], diff[:], ACT.Sigmoid, scale=-1.0)
+
+        def put_a(t):
+            res[t] = work.tile([P, H], F32, name="res")
+            nc.vector.tensor_tensor(res[t][:].indirect(n3_sb[:]), pa2[t][:], sa[t][:], ALU.mult)
+
+        def put_b(t):
+            nc.vector.tensor_tensor(res[t][:].indirect(n4_sb[:]), pb2[t][:], sb[t][:], ALU.mult)
+            nc.sync.dma_start(out_rows[t], res[t][:])
+
+        for t in range(PACK):
+            fetch(pa2, t, hs[t], n3_sb, "pa2")
+            if t > 0:
+                duel(t - 1)
+            fetch(pb2, t, hs[t], n4_sb, "pb2")
+        put_a(0)
+        duel(PACK - 1)
+        put_a(1)
+        put_b(0)
+        put_b(1)
+        put_a(2)
+        put_a(3)
+        put_b(2)
+        put_b(3)

@@ -1,6 +1,7 @@
 from contextlib import ExitStack
 
 import concourse.mybir as mybir
+from concourse.masks import make_identity
 
 F32 = mybir.dt.float32
 BF16 = mybir.dt.bfloat16
@@ -16,7 +17,7 @@ P = 128
 PACK = 4
 T, S, H, N, W = 2048, 512, 512, 512, 256
 HALF = H // 2
-VECTOR_COLS = 96
+VECTOR_COLS = 160
 FLOPS = 2 * 512 * S * H + 2 * S * N * H
 
 
@@ -24,8 +25,8 @@ def tile_picked_tokfillduel_none_p_kernel(tc, x_words, x_scales, wa, gt, w1, off
     nc = tc.nc
     with ExitStack() as ctx:
         keep = ctx.enter_context(tc.tile_pool(name="keep", bufs=1))
-        rows = ctx.enter_context(tc.tile_pool(name="rows", bufs=3))
         work = ctx.enter_context(tc.tile_pool(name="work", bufs=4))
+        reuse = ctx.enter_context(tc.tile_pool(name="reuse", bufs=1))
         psum = ctx.enter_context(tc.psum_pool(name="psum", bufs=8))
 
         x_bytes = keep.tile([P, T], U8, align_bytes=64)
@@ -36,6 +37,8 @@ def tile_picked_tokfillduel_none_p_kernel(tc, x_words, x_scales, wa, gt, w1, off
         warm_out = keep.tile([P, 8], F32)
         nc.vector.memset(warm_in[:], 0.0)
         nc.scalar.activation(warm_out[:], warm_in[:], ACT.Sigmoid)
+        ident = keep.tile([P, P], F32)
+        make_identity(nc, ident[:])
 
         def load_list(dram, name):
             tile = keep.tile(list(dram.shape), U16, name=name)
@@ -45,32 +48,29 @@ def tile_picked_tokfillduel_none_p_kernel(tc, x_words, x_scales, wa, gt, w1, off
         offs_sb = load_list(offs, "offs_sb")
         x_codes = keep.tile([P, T], U32, align_bytes=64)
         nc.sync.dma_start(x_codes[:].bitcast(I32), x_words[0].rearrange("p c r -> p (c r)").bitcast(I32))
+        n1_sb = load_list(n1, "n1_sb")
+        n2_sb = load_list(n2, "n2_sb")
         wa_rows = wa.rearrange("(p j) n -> p j n", j=PACK)
         wa_raw = []
         for u in range(2):
-            raw = keep.tile([P, PACK, HALF], F32, name="wa_raw%d" % u)
+            raw = keep.tile([P, PACK, HALF], F32, align_bytes=64, name="wa_raw%d" % u)
             nc.sync.dma_start(raw[:], wa_rows[:, :, u * HALF : (u + 1) * HALF])
             wa_raw.append(raw)
-        n1_sb = load_list(n1, "n1_sb")
-        n2_sb = load_list(n2, "n2_sb")
-        gt_sb = keep.tile([P, PACK], F32)
-        nc.sync.dma_start(gt_sb[:], gt.rearrange("(p t) o -> p (t o)", t=PACK))
-        w1_raw = keep.tile([P, PACK, N], F32)
-        nc.sync.dma_start(w1_raw[:], w1.rearrange("(p j) n -> p j n", j=PACK))
         n3_sb = load_list(n3, "n3_sb")
         n4_sb = load_list(n4, "n4_sb")
 
-        tok_codes = keep.tile([P, S], U32, align_bytes=64)
-        nc.vector.tensor_copy(tok_codes[:].rearrange("p (t m) -> p m t", t=PACK), x_codes[:].indirect(offs_sb[:]))
-        picked_bytes = keep.tile([P, S], U8, align_bytes=64)
+        picked_bytes = keep.tile([P, S], U8, align_bytes=64, tag="picked")
         nc.vector.tensor_copy(picked_bytes[:], x_bytes[:].indirect(offs_sb[:]))
         tok_bytes = keep.tile([P, S], U8, align_bytes=64)
         nc.vector.tensor_copy(
             tok_bytes[:].rearrange("p (t m) -> p m t", t=PACK), picked_bytes[:].rearrange("p (m t) -> p m t", t=PACK)
         )
+        tok_codes = keep.tile([P, S], U32, align_bytes=64, tag="picked")
+        nc.vector.tensor_copy(tok_codes[:].rearrange("p (t m) -> p m t", t=PACK), x_codes[:].indirect(offs_sb[:]))
 
         wa_codes = keep.tile([P, H], U32, align_bytes=64)
         wa_bytes = keep.tile([P, H], U8, align_bytes=64)
+        wa_grouped = []
         for u in range(2):
             grouped = keep.tile([P, HALF, PACK], BF16, align_bytes=64, name="wa_grouped%d" % u)
             dst = grouped[:].rearrange("p (c i) j -> p c j i", i=4)
@@ -79,125 +79,162 @@ def tile_picked_tokfillduel_none_p_kernel(tc, x_words, x_scales, wa, gt, w1, off
             nc.scalar.copy(dst[:, cut:], src[:, cut:])
             if cut:
                 nc.vector.tensor_copy(dst[:, :cut], src[:, :cut])
+            wa_grouped.append(grouped)
+        for u in range(2):
             cols = slice(u * HALF, (u + 1) * HALF)
             nc.vector.quantize_mx(
-                out=wa_codes[:, cols].bitcast(FP8X4), scales=wa_bytes[:, cols], in_=grouped[:].rearrange("p n j -> p (n j)")
+                out=wa_codes[:, cols].bitcast(FP8X4),
+                scales=wa_bytes[:, cols],
+                in_=wa_grouped[u][:].rearrange("p n j -> p (n j)"),
             )
 
-        def product(dst, lhs_codes, lhs_bytes, rhs_codes, rhs_bytes, pieces):
-            width = H // pieces
-            for u in range(pieces):
-                cols = slice(u * width, (u + 1) * width)
-                acc = psum.tile([P, width], F32, name="acc")
-                nc.tensor.matmul_mx(
-                    out=acc[:],
-                    lhsT=lhs_codes.bitcast(FP8X4),
-                    lhsT_scale=lhs_bytes,
-                    rhs=rhs_codes[:, cols].bitcast(FP8X4),
-                    rhs_scale=rhs_bytes[:, cols],
-                    start=True,
-                    stop=True,
-                )
-                nc.scalar.copy(dst[:, cols], acc[:])
+        w1_raw = reuse.tile([P, PACK, N], F32, align_bytes=64, offset=0)
+        nc.sync.dma_start(w1_raw[:], w1.rearrange("(p j) n -> p j n", j=PACK))
+        gt_sb = keep.tile([P, PACK], F32, align_bytes=64, tag="wa_grouped0")
+        nc.sync.dma_start(gt_sb[:], gt.rearrange("(p t) o -> p (t o)", t=PACK))
 
-        z_grouped = [keep.tile([P, HALF, PACK], BF16, align_bytes=64, name="z_grouped%d" % u) for u in range(2)]
-        w1_grouped = keep.tile([P, PACK, P, PACK], BF16, align_bytes=64)
-        w1_codes = keep.tile([P, N], U32, align_bytes=64)
-        w1_bytes = keep.tile([P, N], U8, align_bytes=64)
-
-        def quantize_w1(t0, t1):
-            cols = slice(t0 * P, t1 * P)
-            nc.vector.quantize_mx(
-                out=w1_codes[:, cols].bitcast(FP8X4),
-                scales=w1_bytes[:, cols],
-                in_=w1_grouped[:, t0:t1].rearrange("p t m j -> p (t m j)"),
-            )
-
-        order = (2, 0, 1, 3)
-        ys, pas, pbs, ras = {}, {}, {}, {}
-
-        def project(t, pieces):
-            cols = slice(t * P, (t + 1) * P)
-            ys[t] = rows.tile([P, H], F32, name="y")
-            product(ys[t], tok_codes[:, cols], tok_bytes[:, cols], wa_codes, wa_bytes, pieces)
-
-        def fetch(store, t, window, offsets, name):
-            store[t] = work.tile([P, W], F32, name=name)
-            nc.vector.tensor_copy(store[t][:], window[:].indirect(offsets[:]))
-
-        def larger(t):
-            ras[t] = work.tile([P, W], F32, name="ra")
-            nc.vector.tensor_tensor(ras[t][:], pas[t][:], pbs[t][:], ALU.max)
-
-        def put_larger(t):
-            nc.vector.tensor_copy(ys[t][:].indirect(n1_sb[:]), ras[t][:])
-
-        def weigh(t, vector_halves):
-            gain = gt_sb[:, t : t + 1]
+        def products(tiles, vector_helps, name, lhs_codes, lhs_bytes, rhs_codes, rhs_bytes):
+            results = {t: keep.tile([P, H], F32, align_bytes=64, name="%s%d" % (name, t)) for t in tiles}
             for u in range(2):
-                src = ys[t][:, u * HALF : (u + 1) * HALF]
-                if u < vector_halves:
-                    nc.vector.tensor_scalar(z_grouped[u][:, :, t], src, gain, None, ALU.mult)
-                else:
-                    nc.scalar.activation(z_grouped[u][:, :, t], src, ACT.Copy, scale=gain)
+                cols = slice(u * HALF, (u + 1) * HALF)
+                for t in tiles:
+                    acc = psum.tile([P, HALF], F32, name="acc")
+                    nc.tensor.matmul_mx(
+                        out=acc[:],
+                        lhsT=lhs_codes[t].bitcast(FP8X4),
+                        lhsT_scale=lhs_bytes[t],
+                        rhs=rhs_codes[:, cols].bitcast(FP8X4),
+                        rhs_scale=rhs_bytes[:, cols],
+                        start=True,
+                        stop=True,
+                    )
+                    if vector_helps and u == 0 and t == tiles[1]:
+                        nc.vector.tensor_copy(results[t][:, cols], acc[:])
+                    else:
+                        nc.scalar.copy(results[t][:, cols], acc[:])
+            return results
 
-        a, b, c, d = order
-        project(a, 2)
-        project(b, 1)
-        project(c, 1)
-        fetch(pas, a, ys[a], n1_sb, "pa")
-        fetch(pbs, a, ys[a], n2_sb, "pb")
-        fetch(pas, b, ys[b], n1_sb, "pa")
-        larger(a)
-        fetch(pbs, b, ys[b], n2_sb, "pb")
-        put_larger(a)
-        weigh(a, 0)
-        project(d, 1)
-        for v in range(4):
+        w1_grouped = keep.tile([P, PACK, P, PACK], BF16, align_bytes=64)
+        w1_codes, w1_bytes = {}, {}
+
+        def group_w1(v):
             ms = slice(v * P // 4, (v + 1) * P // 4)
             nc.scalar.copy(
                 w1_grouped[:].rearrange("p t m j -> p m j t")[:, ms],
                 w1_raw[:].rearrange("p j (m t) -> p m j t", t=PACK)[:, ms],
             )
-        larger(b)
-        fetch(pas, c, ys[c], n1_sb, "pa")
+
+        def quantize_w1(t0, t1, slot, byte_slot):
+            codes = keep.tile([P, (t1 - t0) * P], U32, align_bytes=64, name="w1_codes%d" % t0, tag=slot)
+            scales = keep.tile([P, (t1 - t0) * P], U8, align_bytes=64, name="w1_bytes%d" % t0, tag=byte_slot)
+            nc.vector.quantize_mx(
+                out=codes[:].bitcast(FP8X4), scales=scales[:], in_=w1_grouped[:, t0:t1].rearrange("p t m j -> p (t m j)")
+            )
+            for t in range(t0, t1):
+                cols = slice((t - t0) * P, (t - t0 + 1) * P)
+                w1_codes[t], w1_bytes[t] = codes[:, cols], scales[:, cols]
+
+        pas, ups = {}, {}
+
+        def fetch_pa(t):
+            pas[t] = keep.tile([P, W], F32, align_bytes=64, name="pa%d" % t)
+            nc.vector.tensor_copy(pas[t][:], ys[t][:].indirect(n1_sb[:]))
+
+        def excess(t, up):
+            diff = work.tile([P, W], F32, name="diff")
+            nc.vector.tensor_tensor(diff[:], ys[t][:].indirect(n2_sb[:]), pas[t][:], ALU.subtract)
+            ups[t] = up
+            nc.scalar.activation(ups[t][:], diff[:], ACT.Relu)
+
+        def put_larger(t):
+            nc.vector.tensor_tensor(ys[t][:].indirect(n1_sb[:]), pas[t][:], ups[t][:], ALU.add)
+
+        def weigh(t, vector_cols):
+            gain = gt_sb[:, t : t + 1]
+            if vector_cols:
+                nc.vector.tensor_scalar(z_all[:, :vector_cols, t], ys[t][:, :vector_cols], gain, None, ALU.mult)
+            nc.scalar.activation(z_all[:, vector_cols:, t], ys[t][:, vector_cols:], ACT.Copy, scale=gain)
+
+        a, b, c, d = 2, 0, 1, 3
+        tok_code_tiles = [tok_codes[:, t * P : (t + 1) * P] for t in range(PACK)]
+        tok_byte_tiles = [tok_bytes[:, t * P : (t + 1) * P] for t in range(PACK)]
+        ys = {}
+        for pair in ((a, b), (c, d)):
+            made = products(pair, a in pair, "y", tok_code_tiles, tok_byte_tiles, wa_codes, wa_bytes)
+            for t in pair:
+                ys[t] = made[t]
+        fetch_pa(a)
+        fetch_pa(b)
+        excess(a, keep.tile([P, W], F32, name="up_a"))
+        excess(b, keep.tile([P, W], F32, name="up_b"))
+        for v in range(4):
+            group_w1(v)
+        fetch_pa(c)
+        fetch_pa(d)
+        excess(c, reuse.tile([P, W], F32, name="up_c", offset=4096))
+        excess(d, reuse.tile([P, W], F32, name="up_d", offset=5120))
+        z_all = reuse.tile([P, H, PACK], BF16, align_bytes=64, offset=0)
+        z_grouped = [z_all[:, u * HALF : (u + 1) * HALF] for u in range(2)]
+        put_larger(a)
+        nc.scalar.activation(
+            z_all[:, :, a : a + 2],
+            ys[a][:].unsqueeze(2).to_broadcast([P, H, 2]),
+            ACT.Copy,
+            scale=gt_sb[:, a : a + 1],
+        )
         put_larger(b)
         weigh(b, 0)
-        fetch(pbs, c, ys[c], n2_sb, "pb")
-        fetch(pas, d, ys[d], n1_sb, "pa")
-        larger(c)
-        fetch(pbs, d, ys[d], n2_sb, "pb")
         put_larger(c)
         weigh(c, 0)
-        larger(d)
-        quantize_w1(0, 1)
         put_larger(d)
-        quantize_w1(1, 2)
-        weigh(d, 1)
+        quantize_w1(0, 1, "pa%d" % c, "w1_bytes0")
+        weigh(d, HALF)
+        quantize_w1(1, 2, "y%d" % a, "w1_bytes1")
 
         z_codes = keep.tile([P, H], U32, align_bytes=64)
         z_bytes = keep.tile([P, H], U8, align_bytes=64)
         for u in range(2):
             cols = slice(u * HALF, (u + 1) * HALF)
             nc.vector.quantize_mx(
-                out=z_codes[:, cols].bitcast(FP8X4), scales=z_bytes[:, cols], in_=z_grouped[u][:].rearrange("p n j -> p (n j)")
+                out=z_codes[:, cols].bitcast(FP8X4), scales=z_bytes[:, cols], in_=z_grouped[u].rearrange("p n j -> p (n j)")
             )
-        quantize_w1(2, 4)
+        quantize_w1(2, 4, "y%d" % d, "w1_bytes2")
 
         out_rows = out.rearrange("(p t) n -> t p n", t=PACK)
         hs, pa2, pb2, sa, sb, res = {}, {}, {}, {}, {}, {}
-        for t in range(PACK):
-            cols = slice(t * P, (t + 1) * P)
-            hs[t] = work.tile([P, H], F32, name="h")
-            product(hs[t], w1_codes[:, cols], w1_bytes[:, cols], z_codes, z_bytes, 2 if t == 0 else 1)
+        for pair in ((0, 1), (2, 3)):
+            made = products(pair, 0 in pair, "h", w1_codes, w1_bytes, z_codes, z_bytes)
+            for t in pair:
+                hs[t] = made[t]
+
+        def fetch_pa2(t):
+            pa2[t] = work.tile([P, W], F32, name="pa2")
+            nc.vector.tensor_copy(pa2[t][:], hs[t][:].indirect(n3_sb[:]))
+
+        leads = {}
 
         def duel(t):
-            diff = work.tile([P, W], F32, name="diff")
+            leads[t] = work.tile([P, W], F32, name="lead")
             sa[t] = work.tile([P, W], F32, name="sa")
             sb[t] = work.tile([P, W], F32, name="sb")
-            nc.vector.tensor_tensor(diff[:], pa2[t][:], pb2[t][:], ALU.subtract)
-            nc.scalar.activation(sa[t][:], diff[:], ACT.Sigmoid)
-            nc.scalar.activation(sb[t][:], diff[:], ACT.Sigmoid, scale=-1.0)
+            nc.vector.tensor_tensor(leads[t][:], hs[t][:].indirect(n4_sb[:]), pa2[t][:], ALU.subtract)
+            nc.scalar.activation(sa[t][:], leads[t][:], ACT.Sigmoid, scale=-1.0)
+            nc.scalar.activation(sb[t][:], leads[t][:], ACT.Sigmoid)
+
+        def rebuild_pb2(t):
+            summed = psum.tile([P, W], F32, name="acc")
+            for u in range(W // P):
+                cols = slice(u * P, (u + 1) * P)
+                nc.tensor.matmul(summed[:, cols], pa2[t][:, cols], ident[:], start=True, stop=False, is_transpose=True)
+                nc.tensor.matmul(summed[:, cols], leads[t][:, cols], ident[:], start=False, stop=True, is_transpose=True)
+            turned = work.tile([P, W], F32, name="turned")
+            nc.scalar.copy(turned[:], summed[:])
+            back = psum.tile([P, W], F32, name="acc")
+            for u in range(W // P):
+                cols = slice(u * P, (u + 1) * P)
+                nc.tensor.transpose(back[:, cols], turned[:, cols], ident[:])
+            pb2[t] = work.tile([P, W], F32, name="pb2")
+            nc.scalar.copy(pb2[t][:], back[:])
 
         def put_a(t):
             res[t] = work.tile([P, H], F32, name="res")
@@ -207,17 +244,15 @@ def tile_picked_tokfillduel_none_p_kernel(tc, x_words, x_scales, wa, gt, w1, off
             nc.vector.tensor_tensor(res[t][:].indirect(n4_sb[:]), pb2[t][:], sb[t][:], ALU.mult)
             nc.sync.dma_start(out_rows[t], res[t][:])
 
+        for pair in ((0, 1), (2, 3)):
+            for t in pair:
+                fetch_pa2(t)
+            for t in pair:
+                duel(t)
         for t in range(PACK):
-            fetch(pa2, t, hs[t], n3_sb, "pa2")
-            if t > 0:
-                duel(t - 1)
-            fetch(pb2, t, hs[t], n4_sb, "pb2")
-        put_a(0)
-        duel(PACK - 1)
-        put_a(1)
-        put_b(0)
-        put_b(1)
-        put_a(2)
-        put_a(3)
-        put_b(2)
-        put_b(3)
+            rebuild_pb2(t)
+        for pair in ((0, 1), (2, 3)):
+            for t in pair:
+                put_a(t)
+            for t in pair:
+                put_b(t)

@@ -17,7 +17,7 @@ P = 128
 PACK = 4
 T, S, H, N, W = 2048, 512, 512, 512, 256
 HALF = H // 2
-VECTOR_COLS = 160
+VECTOR_COLS = 96
 FLOPS = 2 * 512 * S * H + 2 * S * N * H
 
 
@@ -38,7 +38,8 @@ def tile_picked_tokfillduel_none_p_kernel(tc, x_words, x_scales, wa, gt, w1, off
         nc.vector.memset(warm_in[:], 0.0)
         nc.scalar.activation(warm_out[:], warm_in[:], ACT.Sigmoid)
         ident = keep.tile([P, P], F32)
-        make_identity(nc, ident[:])
+        nc.vector.memset(ident[:], 0.0)
+        make_identity(nc, ident[:], nomemset=True)
 
         def load_list(dram, name):
             tile = keep.tile(list(dram.shape), U16, name=name)
@@ -59,14 +60,14 @@ def tile_picked_tokfillduel_none_p_kernel(tc, x_words, x_scales, wa, gt, w1, off
         n3_sb = load_list(n3, "n3_sb")
         n4_sb = load_list(n4, "n4_sb")
 
-        picked_bytes = keep.tile([P, S], U8, align_bytes=64, tag="picked")
+        tok_codes = keep.tile([P, S], U32, align_bytes=64)
+        nc.vector.tensor_copy(tok_codes[:].rearrange("p (t m) -> p m t", t=PACK), x_codes[:].indirect(offs_sb[:]))
+        picked_bytes = keep.tile([P, S], U8, align_bytes=64)
         nc.vector.tensor_copy(picked_bytes[:], x_bytes[:].indirect(offs_sb[:]))
         tok_bytes = keep.tile([P, S], U8, align_bytes=64)
         nc.vector.tensor_copy(
             tok_bytes[:].rearrange("p (t m) -> p m t", t=PACK), picked_bytes[:].rearrange("p (m t) -> p m t", t=PACK)
         )
-        tok_codes = keep.tile([P, S], U32, align_bytes=64, tag="picked")
-        nc.vector.tensor_copy(tok_codes[:].rearrange("p (t m) -> p m t", t=PACK), x_codes[:].indirect(offs_sb[:]))
 
         wa_codes = keep.tile([P, H], U32, align_bytes=64)
         wa_bytes = keep.tile([P, H], U8, align_bytes=64)

from contextlib import ExitStack

import concourse.mybir as mybir
from concourse.masks import make_identity

F32 = mybir.dt.float32
BF16 = mybir.dt.bfloat16
I32 = mybir.dt.int32
U32 = mybir.dt.uint32
U16 = mybir.dt.uint16
U8 = mybir.dt.uint8
FP8X4 = mybir.dt.float8_e4m3fn_x4
ALU = mybir.AluOpType
ACT = mybir.ActivationFunctionType

P = 128
PACK = 4
T, S, H, N, W = 2048, 512, 512, 512, 256
HALF = H // 2
VECTOR_COLS = 96
FLOPS = 2 * 512 * S * H + 2 * S * N * H


def tile_picked_tokfillduel_none_p_kernel(tc, x_words, x_scales, wa, gt, w1, offs, n1, n2, n3, n4, out):
    nc = tc.nc
    with ExitStack() as ctx:
        keep = ctx.enter_context(tc.tile_pool(name="keep", bufs=1))
        work = ctx.enter_context(tc.tile_pool(name="work", bufs=4))
        reuse = ctx.enter_context(tc.tile_pool(name="reuse", bufs=1))
        psum = ctx.enter_context(tc.psum_pool(name="psum", bufs=8))

        x_bytes = keep.tile([P, T], U8, align_bytes=64)
        nc.vector.memset(x_bytes[:].bitcast(I32), 0)
        for q in range(4):
            nc.scalar.dma_start(x_bytes[32 * q : 32 * q + 4, :].bitcast(I32), x_scales[0, 4 * q : 4 * q + 4, :].bitcast(I32))
        warm_in = keep.tile([P, 8], F32)
        warm_out = keep.tile([P, 8], F32)
        nc.vector.memset(warm_in[:], 0.0)
        nc.scalar.activation(warm_out[:], warm_in[:], ACT.Sigmoid)
        ident = keep.tile([P, P], F32)
        nc.vector.memset(ident[:], 0.0)
        make_identity(nc, ident[:], nomemset=True)

        def load_list(dram, name):
            tile = keep.tile(list(dram.shape), U16, name=name)
            nc.sync.dma_start(tile[:], dram)
            return tile

        offs_sb = load_list(offs, "offs_sb")
        x_codes = keep.tile([P, T], U32, align_bytes=64)
        nc.sync.dma_start(x_codes[:].bitcast(I32), x_words[0].rearrange("p c r -> p (c r)").bitcast(I32))
        n1_sb = load_list(n1, "n1_sb")
        n2_sb = load_list(n2, "n2_sb")
        wa_rows = wa.rearrange("(p j) n -> p j n", j=PACK)
        wa_raw = []
        for u in range(2):
            raw = keep.tile([P, PACK, HALF], F32, align_bytes=64, name="wa_raw%d" % u)
            nc.sync.dma_start(raw[:], wa_rows[:, :, u * HALF : (u + 1) * HALF])
            wa_raw.append(raw)
        n3_sb = load_list(n3, "n3_sb")
        n4_sb = load_list(n4, "n4_sb")

        tok_codes = keep.tile([P, S], U32, align_bytes=64)
        nc.vector.tensor_copy(tok_codes[:].rearrange("p (t m) -> p m t", t=PACK), x_codes[:].indirect(offs_sb[:]))
        picked_bytes = keep.tile([P, S], U8, align_bytes=64)
        nc.vector.tensor_copy(picked_bytes[:], x_bytes[:].indirect(offs_sb[:]))
        tok_bytes = keep.tile([P, S], U8, align_bytes=64)
        nc.vector.tensor_copy(
            tok_bytes[:].rearrange("p (t m) -> p m t", t=PACK), picked_bytes[:].rearrange("p (m t) -> p m t", t=PACK)
        )

        wa_codes = keep.tile([P, H], U32, align_bytes=64)
        wa_bytes = keep.tile([P, H], U8, align_bytes=64)
        wa_grouped = []
        for u in range(2):
            grouped = keep.tile([P, HALF, PACK], BF16, align_bytes=64, name="wa_grouped%d" % u)
            dst = grouped[:].rearrange("p (c i) j -> p c j i", i=4)
            src = wa_raw[u][:].rearrange("p j (c i) -> p c j i", i=4)
            cut = u * VECTOR_COLS // 4
            nc.scalar.copy(dst[:, cut:], src[:, cut:])
            if cut:
                nc.vector.tensor_copy(dst[:, :cut], src[:, :cut])
            wa_grouped.append(grouped)
        for u in range(2):
            cols = slice(u * HALF, (u + 1) * HALF)
            nc.vector.quantize_mx(
                out=wa_codes[:, cols].bitcast(FP8X4),
                scales=wa_bytes[:, cols],
                in_=wa_grouped[u][:].rearrange("p n j -> p (n j)"),
            )

        w1_raw = reuse.tile([P, PACK, N], F32, align_bytes=64, offset=0)
        nc.sync.dma_start(w1_raw[:], w1.rearrange("(p j) n -> p j n", j=PACK))
        gt_sb = keep.tile([P, PACK], F32, align_bytes=64, tag="wa_grouped0")
        nc.sync.dma_start(gt_sb[:], gt.rearrange("(p t) o -> p (t o)", t=PACK))

        def products(tiles, vector_helps, name, lhs_codes, lhs_bytes, rhs_codes, rhs_bytes):
            results = {t: keep.tile([P, H], F32, align_bytes=64, name="%s%d" % (name, t)) for t in tiles}
            for u in range(2):
                cols = slice(u * HALF, (u + 1) * HALF)
                for t in tiles:
                    acc = psum.tile([P, HALF], F32, name="acc")
                    nc.tensor.matmul_mx(
                        out=acc[:],
                        lhsT=lhs_codes[t].bitcast(FP8X4),
                        lhsT_scale=lhs_bytes[t],
                        rhs=rhs_codes[:, cols].bitcast(FP8X4),
                        rhs_scale=rhs_bytes[:, cols],
                        start=True,
                        stop=True,
                    )
                    if vector_helps and u == 0 and t == tiles[1]:
                        nc.vector.tensor_copy(results[t][:, cols], acc[:])
                    else:
                        nc.scalar.copy(results[t][:, cols], acc[:])
            return results

        w1_grouped = keep.tile([P, PACK, P, PACK], BF16, align_bytes=64)
        w1_codes, w1_bytes = {}, {}

        def group_w1(v):
            ms = slice(v * P // 4, (v + 1) * P // 4)
            nc.scalar.copy(
                w1_grouped[:].rearrange("p t m j -> p m j t")[:, ms],
                w1_raw[:].rearrange("p j (m t) -> p m j t", t=PACK)[:, ms],
            )

        def quantize_w1(t0, t1, slot, byte_slot):
            codes = keep.tile([P, (t1 - t0) * P], U32, align_bytes=64, name="w1_codes%d" % t0, tag=slot)
            scales = keep.tile([P, (t1 - t0) * P], U8, align_bytes=64, name="w1_bytes%d" % t0, tag=byte_slot)
            nc.vector.quantize_mx(
                out=codes[:].bitcast(FP8X4), scales=scales[:], in_=w1_grouped[:, t0:t1].rearrange("p t m j -> p (t m j)")
            )
            for t in range(t0, t1):
                cols = slice((t - t0) * P, (t - t0 + 1) * P)
                w1_codes[t], w1_bytes[t] = codes[:, cols], scales[:, cols]

        pas, ups = {}, {}

        def fetch_pa(t):
            pas[t] = keep.tile([P, W], F32, align_bytes=64, name="pa%d" % t)
            nc.vector.tensor_copy(pas[t][:], ys[t][:].indirect(n1_sb[:]))

        def excess(t, up):
            diff = work.tile([P, W], F32, name="diff")
            nc.vector.tensor_tensor(diff[:], ys[t][:].indirect(n2_sb[:]), pas[t][:], ALU.subtract)
            ups[t] = up
            nc.scalar.activation(ups[t][:], diff[:], ACT.Relu)

        def put_larger(t):
            nc.vector.tensor_tensor(ys[t][:].indirect(n1_sb[:]), pas[t][:], ups[t][:], ALU.add)

        def weigh(t, vector_cols):
            gain = gt_sb[:, t : t + 1]
            if vector_cols:
                nc.vector.tensor_scalar(z_all[:, :vector_cols, t], ys[t][:, :vector_cols], gain, None, ALU.mult)
            nc.scalar.activation(z_all[:, vector_cols:, t], ys[t][:, vector_cols:], ACT.Copy, scale=gain)

        a, b, c, d = 2, 0, 1, 3
        tok_code_tiles = [tok_codes[:, t * P : (t + 1) * P] for t in range(PACK)]
        tok_byte_tiles = [tok_bytes[:, t * P : (t + 1) * P] for t in range(PACK)]
        ys = {}
        for pair in ((a, b), (c, d)):
            made = products(pair, a in pair, "y", tok_code_tiles, tok_byte_tiles, wa_codes, wa_bytes)
            for t in pair:
                ys[t] = made[t]
        fetch_pa(a)
        fetch_pa(b)
        excess(a, keep.tile([P, W], F32, name="up_a"))
        excess(b, keep.tile([P, W], F32, name="up_b"))
        for v in range(4):
            group_w1(v)
        fetch_pa(c)
        fetch_pa(d)
        excess(c, reuse.tile([P, W], F32, name="up_c", offset=4096))
        excess(d, reuse.tile([P, W], F32, name="up_d", offset=5120))
        z_all = reuse.tile([P, H, PACK], BF16, align_bytes=64, offset=0)
        z_grouped = [z_all[:, u * HALF : (u + 1) * HALF] for u in range(2)]
        put_larger(a)
        nc.scalar.activation(
            z_all[:, :, a : a + 2],
            ys[a][:].unsqueeze(2).to_broadcast([P, H, 2]),
            ACT.Copy,
            scale=gt_sb[:, a : a + 1],
        )
        put_larger(b)
        weigh(b, 0)
        put_larger(c)
        weigh(c, 0)
        put_larger(d)
        quantize_w1(0, 1, "pa%d" % c, "w1_bytes0")
        weigh(d, HALF)
        quantize_w1(1, 2, "y%d" % a, "w1_bytes1")

        z_codes = keep.tile([P, H], U32, align_bytes=64)
        z_bytes = keep.tile([P, H], U8, align_bytes=64)
        for u in range(2):
            cols = slice(u * HALF, (u + 1) * HALF)
            nc.vector.quantize_mx(
                out=z_codes[:, cols].bitcast(FP8X4), scales=z_bytes[:, cols], in_=z_grouped[u].rearrange("p n j -> p (n j)")
            )
        quantize_w1(2, 4, "y%d" % d, "w1_bytes2")

        out_rows = out.rearrange("(p t) n -> t p n", t=PACK)
        hs, pa2, pb2, sa, sb, res = {}, {}, {}, {}, {}, {}
        for pair in ((0, 1), (2, 3)):
            made = products(pair, 0 in pair, "h", w1_codes, w1_bytes, z_codes, z_bytes)
            for t in pair:
                hs[t] = made[t]

        def fetch_pa2(t):
            pa2[t] = work.tile([P, W], F32, name="pa2")
            nc.vector.tensor_copy(pa2[t][:], hs[t][:].indirect(n3_sb[:]))

        leads = {}

        def duel(t):
            leads[t] = work.tile([P, W], F32, name="lead")
            sa[t] = work.tile([P, W], F32, name="sa")
            sb[t] = work.tile([P, W], F32, name="sb")
            nc.vector.tensor_tensor(leads[t][:], hs[t][:].indirect(n4_sb[:]), pa2[t][:], ALU.subtract)
            nc.scalar.activation(sa[t][:], leads[t][:], ACT.Sigmoid, scale=-1.0)
            nc.scalar.activation(sb[t][:], leads[t][:], ACT.Sigmoid)

        def rebuild_pb2(t):
            summed = psum.tile([P, W], F32, name="acc")
            for u in range(W // P):
                cols = slice(u * P, (u + 1) * P)
                nc.tensor.matmul(summed[:, cols], pa2[t][:, cols], ident[:], start=True, stop=False, is_transpose=True)
                nc.tensor.matmul(summed[:, cols], leads[t][:, cols], ident[:], start=False, stop=True, is_transpose=True)
            turned = work.tile([P, W], F32, name="turned")
            nc.scalar.copy(turned[:], summed[:])
            back = psum.tile([P, W], F32, name="acc")
            for u in range(W // P):
                cols = slice(u * P, (u + 1) * P)
                nc.tensor.transpose(back[:, cols], turned[:, cols], ident[:])
            pb2[t] = work.tile([P, W], F32, name="pb2")
            nc.scalar.copy(pb2[t][:], back[:])

        def put_a(t):
            res[t] = work.tile([P, H], F32, name="res")
            nc.vector.tensor_tensor(res[t][:].indirect(n3_sb[:]), pa2[t][:], sa[t][:], ALU.mult)

        def put_b(t):
            nc.vector.tensor_tensor(res[t][:].indirect(n4_sb[:]), pb2[t][:], sb[t][:], ALU.mult)
            nc.sync.dma_start(out_rows[t], res[t][:])

        for pair in ((0, 1), (2, 3)):
            for t in pair:
                fetch_pa2(t)
            for t in pair:
                duel(t)
        for t in range(PACK):
            rebuild_pb2(t)
        for pair in ((0, 1), (2, 3)):
            for t in pair:
                put_a(t)
            for t in pair:
                put_b(t)
